import numpy as np, ml_dtypes
CORES = [2,42,66,74,82,90,114]
N = 7
TK = 512
COEF = [[2,-1,0,1,0,0,-1],[-1,2,-1,0,1,0,0],[0,-1,2,-1,0,1,0],[0,0,-1,2,-1,0,1],[1,0,0,-1,2,-1,0],[0,1,0,0,-1,2,-1],[-1,0,1,0,0,-1,2]]
def setup_inputs(rng):
    return {"x": rng.standard_normal((N, 128, TK), dtype=np.float32).astype(ml_dtypes.bfloat16), "a": (rng.standard_normal((N, 128, 128), dtype=np.float32) / 11).astype(ml_dtypes.bfloat16)}
def setup_inputs_big(rng):
    d = setup_inputs(rng)
    for k in ("x", "a"): d[k] = (d[k].astype(np.float32) * 1024.0).astype(d[k].dtype)
    return d
def setup_inputs_small(rng):
    d = setup_inputs(rng)
    for k in ("x", "a"): d[k] = (d[k].astype(np.float32) * (1 / 1024.0)).astype(d[k].dtype)
    return d
def setup_inputs_apart(rng):
    d = setup_inputs(rng)
    f = (10.0 ** rng.permutation(np.linspace(-1.5, 1.5, N))).astype(np.float32).reshape(N, 1, 1)
    for k in ("x", "a"): d[k] = (d[k].astype(np.float32) * f).astype(d[k].dtype)
    return d
def reference(x, a):
    X, A = x.astype(np.float64), a.astype(np.float64)
    y = np.stack([A[r].T @ sum(COEF[r][j] * X[j] for j in range(N)) for r in range(N)])
    return {"y": y.astype(ml_dtypes.bfloat16)}

@@ -1,0 +1,209 @@
+from concourse.bass import DstId, RemoteDMATransfer
+from concourse.mybir import dt, AluOpType
+
+N = 7
+P = 128
+W = 512
+PIECES = [(0, 512)]
+
+
+def ROUTE(j, p, r):
+    return 0
+
+
+SCRATCH = {
+    "xs": ("sbuf", [P, W], "bfloat16"),
+    "a1": ("sbuf", [P, P], "bfloat16"),
+    "cst": ("sbuf", [P, N * P], "bfloat16"),
+    "asc": ("sbuf", [P, N * P], "bfloat16"),
+    "land": ("sbuf", [P, N * W], "bfloat16"),
+    "ys": ("sbuf", [P, W], "bfloat16"),
+}
+for _p in range(len(PIECES)):
+    SCRATCH["ps%d" % _p] = ("psum", [P, 512], "float32")
+
+SEMAPHORES = ["ldx", "lda", "fill", "prep", "sent"]
+for _p in range(len(PIECES)):
+    SEMAPHORES += ["hx%d" % _p, "mm%d" % _p, "cp%d" % _p, "st%d" % _p]
+    SEMAPHORES += ["arr%d_%d" % (_j, _p) for _j in range(N)]
+
+
+def _bits(m):
+    return bin(m).count("1")
+
+
+def _take(m, k):
+    out, e = 0, 0
+    while k > 0:
+        if (m >> e) & 1:
+            out |= 1 << e
+            k -= 1
+        e += 1
+    return out
+
+
+def _pow2(m):
+    k = 1
+    while k * 2 <= _bits(m):
+        k *= 2
+    return _take(m, k)
+
+
+def _helpers(c, cores, topo):
+    away = [d for d in cores if d != c]
+    cand = [h for h in range(topo.CHIPS * topo.CORES_PER_CHIP)
+            if topo.chip(h) == topo.chip(c) and h not in cores and all(topo.may_write(h, d) for d in away)]
+    cand.sort(key=lambda h: (topo.die(h) == topo.die(c), h))
+    return cand
+
+
+def _hops(a, b, topo):
+    ca, cb = topo.chip(a), topo.chip(b)
+    if ca == cb:
+        return 0
+    return 1 if (topo.mates(ca, cb) or topo.same_plane(ca, cb)) else 2
+
+
+def rank_program(g, core, T, topo):
+    cores = list(T.cores)
+    coef = T.tables["COEF"]
+    n = len(cores)
+    sem = T.sem
+    np_ = len(PIECES)
+    helpers = [_helpers(c, cores, topo) for c in cores]
+
+    def needers(j):
+        return [r for r in range(n) if r != j and coef[r][j] != 0]
+
+    def carrier(j, p, r):
+        k = ROUTE(j, p, r)
+        return cores[j] if k == 0 else helpers[j][k - 1]
+
+    def group(j, p, c):
+        return [r for r in needers(j) if carrier(j, p, r) == c]
+
+    def out_mask(c, ranks):
+        m = -1
+        for r in ranks:
+            m &= topo.mask(c, cores[r])
+        return _pow2(m)
+
+    def feed(j, p):
+        hs = sorted(set(carrier(j, p, r) for r in needers(j)) - {cores[j]})
+        if not hs:
+            return hs, 0
+        m = -1
+        for h in hs:
+            m &= topo.mask(cores[j], h)
+        direct = group(j, p, cores[j])
+        if direct:
+            m &= ~out_mask(cores[j], direct)
+        return hs, _pow2(m)
+
+    def ids(cs):
+        out = []
+        for c in cs:
+            rid, pid, _se = topo.addr(c)
+            out.append(DstId(rid=rid, pnc=pid))
+        return out
+
+    def deliver(j, p, ranks, m):
+        lo, hi = PIECES[p]
+        return RemoteDMATransfer(dst_ids=ids([cores[r] for r in ranks]), dma_engine_mask=m,
+                                 remote_sem=sem["arr%d_%d" % (j, p)], srcs=[T.xs[:, lo:hi]],
+                                 dsts=[T.land[:, j * W + lo:j * W + hi] for _r in ranks], alu_op=0)
+
+    rank = T.rank_of(core)
+
+    if rank is None:
+        for j in range(n):
+            if core not in helpers[j]:
+                continue
+            sent = 0
+            for p in range(np_):
+                ranks = group(j, p, core)
+                if not ranks:
+                    continue
+                g.wait_ge(sem["hx%d" % p], _bits(feed(j, p)[1]))
+                m = out_mask(core, ranks)
+                g.remote_dma_fused([deliver(j, p, ranks, m)], local_sem=sem.sent)
+                sent += _bits(m)
+            if sent:
+                g.wait_ge(sem.sent, sent)
+        return
+
+    j = rank
+    g.sync.dma_start(T.xs[:], T.x[:]).then_inc(sem.ldx, 16)
+    g.scalar.dma_start(T.a1[:], T.a[:]).then_inc(sem.lda, 16)
+
+    g.wait_ge(sem.ldx, 16)
+    sent = 0
+    for p in range(np_):
+        lo, hi = PIECES[p]
+        trs = []
+        direct = group(j, p, core)
+        if direct:
+            m = out_mask(core, direct)
+            trs.append(deliver(j, p, direct, m))
+            sent += _bits(m)
+        hs, m = feed(j, p)
+        if hs:
+            trs.append(RemoteDMATransfer(dst_ids=ids(hs), dma_engine_mask=m, remote_sem=sem["hx%d" % p],
+                                         srcs=[T.xs[:, lo:hi]], dsts=[T.xs[:, lo:hi] for _h in hs], alu_op=0))
+            sent += _bits(m)
+        if trs:
+            g.remote_dma_fused(trs, local_sem=sem.sent)
+
+    vals = sorted(set(coef[j][k] for k in range(n) if coef[j][k] not in (0, 1)))
+    for i, c in enumerate(vals):
+        g.vector.memset(T.cst[:, i * P:(i + 1) * P], float(c)).then_inc(sem.fill, 1)
+    if vals:
+        g.vector.wait_ge(sem.fill, len(vals))
+    g.vector.wait_ge(sem.lda, 16)
+    for i, c in enumerate(vals):
+        g.vector.tensor_tensor(T.asc[:, i * P:(i + 1) * P], T.a1[:], T.cst[:, i * P:(i + 1) * P],
+                               AluOpType.mult).then_inc(sem.prep, 1)
+
+    def lhs(c):
+        if c == 1:
+            return T.a1[:]
+        i = vals.index(c)
+        return T.asc[:, i * P:(i + 1) * P]
+
+    srcs = [k for k in range(n) if k != j and coef[j][k] != 0]
+    items = sorted((carrier(k, p, j) != cores[k], p, _hops(cores[k], core, topo), k) for k in srcs for p in range(np_))
+    left = [len(srcs)] * np_
+    g.tensor.wait_ge(sem.ldx, 16)
+    g.tensor.wait_ge(sem.lda, 16)
+    if vals:
+        g.tensor.wait_ge(sem.prep, len(vals))
+    order = []
+    for p in range(np_):
+        lo, hi = PIECES[p]
+        mm = g.tensor.matmul(T["ps%d" % p][:, 0:hi - lo], lhs(coef[j][j]), T.xs[:, lo:hi], True, left[p] == 0)
+        if left[p] == 0:
+            mm.then_inc(sem["mm%d" % p], 1)
+            order.append(p)
+    for _via, p, _h, k in items:
+        lo, hi = PIECES[p]
+        c = carrier(k, p, j)
+        g.tensor.wait_ge(sem["arr%d_%d" % (k, p)], _bits(out_mask(c, group(k, p, c))))
+        left[p] -= 1
+        mm = g.tensor.matmul(T["ps%d" % p][:, 0:hi - lo], lhs(coef[j][k]), T.land[:, k * W + lo:k * W + hi],
+                             False, left[p] == 0)
+        if left[p] == 0:
+            mm.then_inc(sem["mm%d" % p], 1)
+            order.append(p)
+
+    queues = [g.sync, g.scalar]
+    for i, p in enumerate(order):
+        lo, hi = PIECES[p]
+        g.vector.wait_ge(sem["mm%d" % p], 1)
+        g.vector.tensor_copy(T.ys[:, lo:hi], T["ps%d" % p][:, 0:hi - lo]).then_inc(sem["cp%d" % p], 1)
+        q = queues[i % 2]
+        q.wait_ge(sem["cp%d" % p], 1)
+        q.dma_start(T.y[:, lo:hi], T.ys[:, lo:hi]).then_inc(sem["st%d" % p], 16)
+    for i, p in enumerate(order):
+        queues[i % 2].wait_ge(sem["st%d" % p], 16)
+    if sent:
+        g.wait_ge(sem.sent, sent)

@@ -8,7 +8,7 @@ PIECES = [(0, 512)]
 
 
 def ROUTE(j, p, r):
-    return 0
+    return 1 if (r - j) % N == 4 else 0
 
 
 SCRATCH = {
@@ -138,7 +138,7 @@ def rank_program(g, core, T, topo):
 
     g.wait_ge(sem.ldx, 16)
     sent = 0
-    for p in range(np_):
+    for p in sorted(range(np_), key=lambda q: (not feed(j, q)[0], q)):
         lo, hi = PIECES[p]
         trs = []
         direct = group(j, p, core)

@@ -4,11 +4,15 @@ from concourse.mybir import dt, AluOpType
 N = 7
 P = 128
 W = 512
-PIECES = [(0, 512)]
+PIECES = [(0, 256), (256, 512)]
+SAME_DIE = True
+OUT_ENG = 8
+FEED_ENG = 8
+SPLIT_FEED = False
 
 
 def ROUTE(j, p, r):
-    return 1 if (r - j) % N == 4 else 0
+    return 0
 
 
 SCRATCH = {
@@ -22,9 +26,9 @@ SCRATCH = {
 for _p in range(len(PIECES)):
     SCRATCH["ps%d" % _p] = ("psum", [P, 512], "float32")
 
-SEMAPHORES = ["ldx", "lda", "fill", "prep", "sent"]
+SEMAPHORES = ["lda", "fill", "prep", "sent"]
 for _p in range(len(PIECES)):
-    SEMAPHORES += ["hx%d" % _p, "mm%d" % _p, "cp%d" % _p, "st%d" % _p]
+    SEMAPHORES += ["ldx%d" % _p, "hx%d" % _p, "mm%d" % _p, "cp%d" % _p, "st%d" % _p]
     SEMAPHORES += ["arr%d_%d" % (_j, _p) for _j in range(N)]
 
 
@@ -32,28 +36,23 @@ def _bits(m):
     return bin(m).count("1")
 
 
-def _take(m, k):
-    out, e = 0, 0
-    while k > 0:
-        if (m >> e) & 1:
-            out |= 1 << e
-            k -= 1
-        e += 1
-    return out
-
-
-def _pow2(m):
+def _pick(m, cap):
+    on = [e for e in range(m.bit_length()) if (m >> e) & 1]
     k = 1
-    while k * 2 <= _bits(m):
+    while k * 2 <= min(len(on), cap):
         k *= 2
-    return _take(m, k)
+    step = len(on) // k
+    out = 0
+    for i in range(k):
+        out |= 1 << on[i * step]
+    return out
 
 
 def _helpers(c, cores, topo):
     away = [d for d in cores if d != c]
     cand = [h for h in range(topo.CHIPS * topo.CORES_PER_CHIP)
             if topo.chip(h) == topo.chip(c) and h not in cores and all(topo.may_write(h, d) for d in away)]
-    cand.sort(key=lambda h: (topo.die(h) == topo.die(c), h))
+    cand.sort(key=lambda h: ((topo.die(h) == topo.die(c)) != SAME_DIE, h))
     return cand
 
 
@@ -83,22 +82,21 @@ def rank_program(g, core, T, topo):
         return [r for r in needers(j) if carrier(j, p, r) == c]
 
     def out_mask(c, ranks):
-        m = -1
+        m = topo.mask(c, cores[ranks[0]])
         for r in ranks:
             m &= topo.mask(c, cores[r])
-        return _pow2(m)
+        return _pick(m, OUT_ENG)
 
     def feed(j, p):
         hs = sorted(set(carrier(j, p, r) for r in needers(j)) - {cores[j]})
         if not hs:
             return hs, 0
-        m = -1
+        m = topo.mask(cores[j], hs[0])
         for h in hs:
             m &= topo.mask(cores[j], h)
-        direct = group(j, p, cores[j])
-        if direct:
-            m &= ~out_mask(cores[j], direct)
-        return hs, _pow2(m)
+        for r in needers(j):
+            m &= ~topo.mask(cores[j], cores[r])
+        return hs, _pick(m, FEED_ENG)
 
     def ids(cs):
         out = []
@@ -133,23 +131,28 @@ def rank_program(g, core, T, topo):
         return
 
     j = rank
-    g.sync.dma_start(T.xs[:], T.x[:]).then_inc(sem.ldx, 16)
-    g.scalar.dma_start(T.a1[:], T.a[:]).then_inc(sem.lda, 16)
-
-    g.wait_ge(sem.ldx, 16)
-    sent = 0
-    for p in sorted(range(np_), key=lambda q: (not feed(j, q)[0], q)):
+    for p in range(np_):
         lo, hi = PIECES[p]
+        g.sync.dma_start(T.xs[:, lo:hi], T.x[:, lo:hi]).then_inc(sem["ldx%d" % p], 16)
+    g.sync.dma_start(T.a1[:], T.a[:]).then_inc(sem.lda, 16)
+
+    sent = 0
+    for p in range(np_):
+        lo, hi = PIECES[p]
+        g.wait_ge(sem["ldx%d" % p], 16)
         trs = []
-        direct = group(j, p, core)
-        if direct:
-            m = out_mask(core, direct)
-            trs.append(deliver(j, p, direct, m))
-            sent += _bits(m)
         hs, m = feed(j, p)
         if hs:
             trs.append(RemoteDMATransfer(dst_ids=ids(hs), dma_engine_mask=m, remote_sem=sem["hx%d" % p],
                                          srcs=[T.xs[:, lo:hi]], dsts=[T.xs[:, lo:hi] for _h in hs], alu_op=0))
+            sent += _bits(m)
+            if SPLIT_FEED:
+                g.remote_dma_fused(trs, local_sem=sem.sent)
+                trs = []
+        direct = group(j, p, core)
+        if direct:
+            m = out_mask(core, direct)
+            trs.append(deliver(j, p, direct, m))
             sent += _bits(m)
         if trs:
             g.remote_dma_fused(trs, local_sem=sem.sent)
@@ -171,9 +174,10 @@ def rank_program(g, core, T, topo):
         return T.asc[:, i * P:(i + 1) * P]
 
     srcs = [k for k in range(n) if k != j and coef[j][k] != 0]
-    items = sorted((carrier(k, p, j) != cores[k], p, _hops(cores[k], core, topo), k) for k in srcs for p in range(np_))
+    items = sorted((p, carrier(k, p, j) != cores[k], _hops(cores[k], core, topo), k) for k in srcs for p in range(np_))
     left = [len(srcs)] * np_
-    g.tensor.wait_ge(sem.ldx, 16)
+    for p in range(np_):
+        g.tensor.wait_ge(sem["ldx%d" % p], 16)
     g.tensor.wait_ge(sem.lda, 16)
     if vals:
         g.tensor.wait_ge(sem.prep, len(vals))
@@ -184,7 +188,7 @@ def rank_program(g, core, T, topo):
         if left[p] == 0:
             mm.then_inc(sem["mm%d" % p], 1)
             order.append(p)
-    for _via, p, _h, k in items:
+    for p, _via, _h, k in items:
         lo, hi = PIECES[p]
         c = carrier(k, p, j)
         g.tensor.wait_ge(sem["arr%d_%d" % (k, p)], _bits(out_mask(c, group(k, p, c))))

@@ -5,15 +5,6 @@ N = 7
 P = 128
 W = 512
 PIECES = [(0, 256), (256, 512)]
-SAME_DIE = True
-OUT_ENG = 8
-FEED_ENG = 8
-SPLIT_FEED = False
-
-
-def ROUTE(j, p, r):
-    return 0
-
 
 SCRATCH = {
     "xs": ("sbuf", [P, W], "bfloat16"),
@@ -28,7 +19,7 @@ for _p in range(len(PIECES)):
 
 SEMAPHORES = ["lda", "fill", "prep", "sent"]
 for _p in range(len(PIECES)):
-    SEMAPHORES += ["ldx%d" % _p, "hx%d" % _p, "mm%d" % _p, "cp%d" % _p, "st%d" % _p]
+    SEMAPHORES += ["ldx%d" % _p, "mm%d" % _p, "cp%d" % _p, "st%d" % _p]
     SEMAPHORES += ["arr%d_%d" % (_j, _p) for _j in range(N)]
 
 
@@ -36,126 +27,103 @@ def _bits(m):
     return bin(m).count("1")
 
 
-def _pick(m, cap):
-    on = [e for e in range(m.bit_length()) if (m >> e) & 1]
-    k = 1
-    while k * 2 <= min(len(on), cap):
-        k *= 2
-    step = len(on) // k
-    out = 0
-    for i in range(k):
-        out |= 1 << on[i * step]
+def _links(a, b, topo):
+    ca, cb, d = topo.chip(a), topo.chip(b), topo.die(a)
+    out = []
+    if ca == cb:
+        return out
+    if not topo.same_plane(ca, cb):
+        out.append(("mate", ca, d))
+        ca = [c for c in range(topo.CHIPS) if topo.mates(ca, c)][0]
+    if ca != cb:
+        out += [("out", ca, d), ("in", cb, d)]
     return out
 
 
-def _helpers(c, cores, topo):
-    away = [d for d in cores if d != c]
-    cand = [h for h in range(topo.CHIPS * topo.CORES_PER_CHIP)
-            if topo.chip(h) == topo.chip(c) and h not in cores and all(topo.may_write(h, d) for d in away)]
-    cand.sort(key=lambda h: ((topo.die(h) == topo.die(c)) != SAME_DIE, h))
-    return cand
+def _orders(items):
+    if len(items) <= 1:
+        return [list(items)]
+    out = []
+    for i in range(len(items)):
+        out += [[items[i]] + rest for rest in _orders(items[:i] + items[i + 1:])]
+    return out
 
 
-def _hops(a, b, topo):
-    ca, cb = topo.chip(a), topo.chip(b)
-    if ca == cb:
-        return 0
-    return 1 if (topo.mates(ca, cb) or topo.same_plane(ca, cb)) else 2
+def _timetable(cores, coef, topo):
+    n = len(cores)
+    need = [[r for r in range(n) if r != s and coef[r][s] != 0] for s in range(n)]
+    found = []
+
+    def rec(s, used, acc):
+        if s == n:
+            found.append(acc)
+            return
+        for order in _orders(need[s]):
+            add = set()
+            for t, r in enumerate(order):
+                add.add((t, "to", r))
+                for l in _links(cores[s], cores[r], topo):
+                    add.add((t, l))
+            if not (add & used):
+                rec(s + 1, used | add, acc + [order])
+
+    rec(0, set(), [])
+    if not found:
+        return [sorted(need[s], key=lambda r: (r - s) % n) for s in range(n)]
+
+    def weight(tab):
+        turns = max(len(o) for o in tab)
+        return [sum(len(_links(cores[s], cores[o[t]], topo)) for s, o in enumerate(tab) if t < len(o))
+                for t in range(turns)]
+
+    best = found[0]
+    for tab in found[1:]:
+        if weight(tab) > weight(best):
+            best = tab
+    return best
 
 
 def rank_program(g, core, T, topo):
+    rank = T.rank_of(core)
+    if rank is None:
+        return
     cores = list(T.cores)
     coef = T.tables["COEF"]
     n = len(cores)
     sem = T.sem
     np_ = len(PIECES)
-    helpers = [_helpers(c, cores, topo) for c in cores]
+    j = rank
 
-    def needers(j):
-        return [r for r in range(n) if r != j and coef[r][j] != 0]
-
-    def carrier(j, p, r):
-        k = ROUTE(j, p, r)
-        return cores[j] if k == 0 else helpers[j][k - 1]
-
-    def group(j, p, c):
-        return [r for r in needers(j) if carrier(j, p, r) == c]
+    table = _timetable(cores, coef, topo)
+    dsts = table[j]
+    srcs = sorted((k for k in range(n) if j in table[k]), key=lambda k: (table[k].index(j), k))
 
     def out_mask(c, ranks):
         m = topo.mask(c, cores[ranks[0]])
         for r in ranks:
             m &= topo.mask(c, cores[r])
-        return _pick(m, OUT_ENG)
+        return m
 
-    def feed(j, p):
-        hs = sorted(set(carrier(j, p, r) for r in needers(j)) - {cores[j]})
-        if not hs:
-            return hs, 0
-        m = topo.mask(cores[j], hs[0])
-        for h in hs:
-            m &= topo.mask(cores[j], h)
-        for r in needers(j):
-            m &= ~topo.mask(cores[j], cores[r])
-        return hs, _pick(m, FEED_ENG)
-
-    def ids(cs):
-        out = []
-        for c in cs:
-            rid, pid, _se = topo.addr(c)
-            out.append(DstId(rid=rid, pnc=pid))
-        return out
-
-    def deliver(j, p, ranks, m):
-        lo, hi = PIECES[p]
-        return RemoteDMATransfer(dst_ids=ids([cores[r] for r in ranks]), dma_engine_mask=m,
-                                 remote_sem=sem["arr%d_%d" % (j, p)], srcs=[T.xs[:, lo:hi]],
-                                 dsts=[T.land[:, j * W + lo:j * W + hi] for _r in ranks], alu_op=0)
-
-    rank = T.rank_of(core)
-
-    if rank is None:
-        for j in range(n):
-            if core not in helpers[j]:
-                continue
-            sent = 0
-            for p in range(np_):
-                ranks = group(j, p, core)
-                if not ranks:
-                    continue
-                g.wait_ge(sem["hx%d" % p], _bits(feed(j, p)[1]))
-                m = out_mask(core, ranks)
-                g.remote_dma_fused([deliver(j, p, ranks, m)], local_sem=sem.sent)
-                sent += _bits(m)
-            if sent:
-                g.wait_ge(sem.sent, sent)
-        return
-
-    j = rank
     for p in range(np_):
         lo, hi = PIECES[p]
         g.sync.dma_start(T.xs[:, lo:hi], T.x[:, lo:hi]).then_inc(sem["ldx%d" % p], 16)
     g.sync.dma_start(T.a1[:], T.a[:]).then_inc(sem.lda, 16)
 
     sent = 0
-    for p in range(np_):
-        lo, hi = PIECES[p]
-        g.wait_ge(sem["ldx%d" % p], 16)
-        trs = []
-        hs, m = feed(j, p)
-        if hs:
-            trs.append(RemoteDMATransfer(dst_ids=ids(hs), dma_engine_mask=m, remote_sem=sem["hx%d" % p],
-                                         srcs=[T.xs[:, lo:hi]], dsts=[T.xs[:, lo:hi] for _h in hs], alu_op=0))
+    if dsts:
+        m = out_mask(core, dsts)
+        ids = []
+        for r in dsts:
+            rid, pid, _se = topo.addr(cores[r])
+            ids.append(DstId(rid=rid, pnc=pid))
+        for p in range(np_):
+            lo, hi = PIECES[p]
+            g.wait_ge(sem["ldx%d" % p], 16)
+            g.remote_dma_fused([RemoteDMATransfer(dst_ids=ids, dma_engine_mask=m, remote_sem=sem["arr%d_%d" % (j, p)],
+                                                  srcs=[T.xs[:, lo:hi]],
+                                                  dsts=[T.land[:, j * W + lo:j * W + hi] for _r in dsts], alu_op=0)],
+                               local_sem=sem.sent)
             sent += _bits(m)
-            if SPLIT_FEED:
-                g.remote_dma_fused(trs, local_sem=sem.sent)
-                trs = []
-        direct = group(j, p, core)
-        if direct:
-            m = out_mask(core, direct)
-            trs.append(deliver(j, p, direct, m))
-            sent += _bits(m)
-        if trs:
-            g.remote_dma_fused(trs, local_sem=sem.sent)
 
     vals = sorted(set(coef[j][k] for k in range(n) if coef[j][k] not in (0, 1)))
     for i, c in enumerate(vals):
@@ -173,41 +141,34 @@ def rank_program(g, core, T, topo):
         i = vals.index(c)
         return T.asc[:, i * P:(i + 1) * P]
 
-    srcs = [k for k in range(n) if k != j and coef[j][k] != 0]
-    items = sorted((p, carrier(k, p, j) != cores[k], _hops(cores[k], core, topo), k) for k in srcs for p in range(np_))
-    left = [len(srcs)] * np_
     for p in range(np_):
         g.tensor.wait_ge(sem["ldx%d" % p], 16)
     g.tensor.wait_ge(sem.lda, 16)
     if vals:
         g.tensor.wait_ge(sem.prep, len(vals))
-    order = []
     for p in range(np_):
         lo, hi = PIECES[p]
-        mm = g.tensor.matmul(T["ps%d" % p][:, 0:hi - lo], lhs(coef[j][j]), T.xs[:, lo:hi], True, left[p] == 0)
-        if left[p] == 0:
+        mm = g.tensor.matmul(T["ps%d" % p][:, 0:hi - lo], lhs(coef[j][j]), T.xs[:, lo:hi], True, not srcs)
+        if not srcs:
             mm.then_inc(sem["mm%d" % p], 1)
-            order.append(p)
-    for p, _via, _h, k in items:
+    for p in range(np_):
         lo, hi = PIECES[p]
-        c = carrier(k, p, j)
-        g.tensor.wait_ge(sem["arr%d_%d" % (k, p)], _bits(out_mask(c, group(k, p, c))))
-        left[p] -= 1
-        mm = g.tensor.matmul(T["ps%d" % p][:, 0:hi - lo], lhs(coef[j][k]), T.land[:, k * W + lo:k * W + hi],
-                             False, left[p] == 0)
-        if left[p] == 0:
-            mm.then_inc(sem["mm%d" % p], 1)
-            order.append(p)
+        for k in srcs:
+            g.tensor.wait_ge(sem["arr%d_%d" % (k, p)], _bits(out_mask(cores[k], table[k])))
+            mm = g.tensor.matmul(T["ps%d" % p][:, 0:hi - lo], lhs(coef[j][k]), T.land[:, k * W + lo:k * W + hi],
+                                 False, k == srcs[-1])
+            if k == srcs[-1]:
+                mm.then_inc(sem["mm%d" % p], 1)
 
     queues = [g.sync, g.scalar]
-    for i, p in enumerate(order):
+    for p in range(np_):
         lo, hi = PIECES[p]
         g.vector.wait_ge(sem["mm%d" % p], 1)
         g.vector.tensor_copy(T.ys[:, lo:hi], T["ps%d" % p][:, 0:hi - lo]).then_inc(sem["cp%d" % p], 1)
-        q = queues[i % 2]
+        q = queues[p % 2]
         q.wait_ge(sem["cp%d" % p], 1)
         q.dma_start(T.y[:, lo:hi], T.ys[:, lo:hi]).then_inc(sem["st%d" % p], 16)
-    for i, p in enumerate(order):
-        queues[i % 2].wait_ge(sem["st%d" % p], 16)
+    for p in range(np_):
+        queues[p % 2].wait_ge(sem["st%d" % p], 16)
     if sent:
         g.wait_ge(sem.sent, sent)

from concourse.bass import DstId, RemoteDMATransfer
from concourse.mybir import dt, AluOpType

N = 7
P = 128
W = 512
PIECES = [(0, 256), (256, 512)]

SCRATCH = {
    "xs": ("sbuf", [P, W], "bfloat16"),
    "a1": ("sbuf", [P, P], "bfloat16"),
    "cst": ("sbuf", [P, N * P], "bfloat16"),
    "asc": ("sbuf", [P, N * P], "bfloat16"),
    "land": ("sbuf", [P, N * W], "bfloat16"),
    "ys": ("sbuf", [P, W], "bfloat16"),
}
for _p in range(len(PIECES)):
    SCRATCH["ps%d" % _p] = ("psum", [P, 512], "float32")

SEMAPHORES = ["lda", "fill", "prep", "sent"]
for _p in range(len(PIECES)):
    SEMAPHORES += ["ldx%d" % _p, "mm%d" % _p, "cp%d" % _p, "st%d" % _p]
    SEMAPHORES += ["arr%d_%d" % (_j, _p) for _j in range(N)]


def _bits(m):
    return bin(m).count("1")


def _links(a, b, topo):
    ca, cb, d = topo.chip(a), topo.chip(b), topo.die(a)
    out = []
    if ca == cb:
        return out
    if not topo.same_plane(ca, cb):
        out.append(("mate", ca, d))
        ca = [c for c in range(topo.CHIPS) if topo.mates(ca, c)][0]
    if ca != cb:
        out += [("out", ca, d), ("in", cb, d)]
    return out


def _orders(items):
    if len(items) <= 1:
        return [list(items)]
    out = []
    for i in range(len(items)):
        out += [[items[i]] + rest for rest in _orders(items[:i] + items[i + 1:])]
    return out


def _timetable(cores, coef, topo):
    n = len(cores)
    need = [[r for r in range(n) if r != s and coef[r][s] != 0] for s in range(n)]
    found = []

    def rec(s, used, acc):
        if s == n:
            found.append(acc)
            return
        for order in _orders(need[s]):
            add = set()
            for t, r in enumerate(order):
                add.add((t, "to", r))
                for l in _links(cores[s], cores[r], topo):
                    add.add((t, l))
            if not (add & used):
                rec(s + 1, used | add, acc + [order])

    rec(0, set(), [])
    if not found:
        return [sorted(need[s], key=lambda r: (r - s) % n) for s in range(n)]

    def weight(tab):
        turns = max(len(o) for o in tab)
        return [sum(len(_links(cores[s], cores[o[t]], topo)) for s, o in enumerate(tab) if t < len(o))
                for t in range(turns)]

    best = found[0]
    for tab in found[1:]:
        if weight(tab) > weight(best):
            best = tab
    return best


def rank_program(g, core, T, topo):
    rank = T.rank_of(core)
    if rank is None:
        return
    cores = list(T.cores)
    coef = T.tables["COEF"]
    n = len(cores)
    sem = T.sem
    np_ = len(PIECES)
    j = rank

    table = _timetable(cores, coef, topo)
    dsts = table[j]
    srcs = sorted((k for k in range(n) if j in table[k]), key=lambda k: (table[k].index(j), k))

    def out_mask(c, ranks):
        m = topo.mask(c, cores[ranks[0]])
        for r in ranks:
            m &= topo.mask(c, cores[r])
        return m

    for p in range(np_):
        lo, hi = PIECES[p]
        g.sync.dma_start(T.xs[:, lo:hi], T.x[:, lo:hi]).then_inc(sem["ldx%d" % p], 16)
    g.sync.dma_start(T.a1[:], T.a[:]).then_inc(sem.lda, 16)

    sent = 0
    if dsts:
        m = out_mask(core, dsts)
        ids = []
        for r in dsts:
            rid, pid, _se = topo.addr(cores[r])
            ids.append(DstId(rid=rid, pnc=pid))
        for p in range(np_):
            lo, hi = PIECES[p]
            g.wait_ge(sem["ldx%d" % p], 16)
            g.remote_dma_fused([RemoteDMATransfer(dst_ids=ids, dma_engine_mask=m, remote_sem=sem["arr%d_%d" % (j, p)],
                                                  srcs=[T.xs[:, lo:hi]],
                                                  dsts=[T.land[:, j * W + lo:j * W + hi] for _r in dsts], alu_op=0)],
                               local_sem=sem.sent)
            sent += _bits(m)

    vals = sorted(set(coef[j][k] for k in range(n) if coef[j][k] not in (0, 1)))
    for i, c in enumerate(vals):
        g.vector.memset(T.cst[:, i * P:(i + 1) * P], float(c)).then_inc(sem.fill, 1)
    if vals:
        g.vector.wait_ge(sem.fill, len(vals))
    g.vector.wait_ge(sem.lda, 16)
    for i, c in enumerate(vals):
        g.vector.tensor_tensor(T.asc[:, i * P:(i + 1) * P], T.a1[:], T.cst[:, i * P:(i + 1) * P],
                               AluOpType.mult).then_inc(sem.prep, 1)

    def lhs(c):
        if c == 1:
            return T.a1[:]
        i = vals.index(c)
        return T.asc[:, i * P:(i + 1) * P]

    for p in range(np_):
        g.tensor.wait_ge(sem["ldx%d" % p], 16)
    g.tensor.wait_ge(sem.lda, 16)
    if vals:
        g.tensor.wait_ge(sem.prep, len(vals))
    for p in range(np_):
        lo, hi = PIECES[p]
        mm = g.tensor.matmul(T["ps%d" % p][:, 0:hi - lo], lhs(coef[j][j]), T.xs[:, lo:hi], True, not srcs)
        if not srcs:
            mm.then_inc(sem["mm%d" % p], 1)
    for p in range(np_):
        lo, hi = PIECES[p]
        for k in srcs:
            g.tensor.wait_ge(sem["arr%d_%d" % (k, p)], _bits(out_mask(cores[k], table[k])))
            mm = g.tensor.matmul(T["ps%d" % p][:, 0:hi - lo], lhs(coef[j][k]), T.land[:, k * W + lo:k * W + hi],
                                 False, k == srcs[-1])
            if k == srcs[-1]:
                mm.then_inc(sem["mm%d" % p], 1)

    queues = [g.sync, g.scalar]
    for p in range(np_):
        lo, hi = PIECES[p]
        g.vector.wait_ge(sem["mm%d" % p], 1)
        g.vector.tensor_copy(T.ys[:, lo:hi], T["ps%d" % p][:, 0:hi - lo]).then_inc(sem["cp%d" % p], 1)
        q = queues[p % 2]
        q.wait_ge(sem["cp%d" % p], 1)
        q.dma_start(T.y[:, lo:hi], T.ys[:, lo:hi]).then_inc(sem["st%d" % p], 16)
    for p in range(np_):
        queues[p % 2].wait_ge(sem["st%d" % p], 16)
    if sent:
        g.wait_ge(sem.sent, sent)
